import numpy as np
import ml_dtypes


def mxq(x, axis, fmt="e4m3"):
    dtype, down = {"e4m3": (ml_dtypes.float8_e4m3fn, 7), "e5m2": (ml_dtypes.float8_e5m2, 14)}[fmt]
    v = np.moveaxis(np.asarray(x, np.float32).astype(ml_dtypes.bfloat16).astype(np.float64), axis, -1)
    blocks = v.reshape(v.shape[:-1] + (-1, 32))
    amax = np.abs(blocks).max(-1, keepdims=True)
    byte = np.maximum(np.where(amax > 0, np.frexp(amax)[1] - 1 + 127, 0) - down, 1)
    scale = np.exp2(byte - 127.0)
    codes = (blocks / scale).astype(np.float32).astype(dtype).astype(np.float64)
    return np.moveaxis((codes * scale).reshape(v.shape), -1, axis)


WIDE = False


def mx_kscale(k):
    if not WIDE:
        return np.ones(k)
    levels = np.array([24, -24, 12, -12, 0])
    if k % 512:
        return np.exp2(np.random.permutation(np.resize(levels, k // 32))).repeat(32)
    a = np.empty((k // 512, 16))
    for p in range(k // 512):
        a[p, :8] = np.random.permutation(np.resize(levels, 8))
        for g in range(8):
            far = levels[np.abs(levels - a[p, g]) >= 10]
            a[p, g + 8] = far[np.random.randint(len(far))]
    return np.exp2(a.ravel()).repeat(32)


def f64(x):
    return np.asarray(x).astype(np.float64)


def striped(idx):
    return np.tile(idx.reshape(-1, 16).T, (8, 1)).astype(np.uint16)


def unstriped(offs):
    return offs[:16].T.reshape(-1).astype(np.int64)


E2M1 = np.array([0.0, 0.5, 1.0, 1.5, 2.0, 3.0, 4.0, 6.0, -0.0, -0.5, -1.0, -1.5, -2.0, -3.0, -4.0, -6.0])


def pack_weight(w, fmt):
    k, n = w.shape
    w = f64(np.asarray(w, np.float32).astype(ml_dtypes.bfloat16)).reshape(k // 32, 32, n)
    amax = np.abs(w).max(1)
    if fmt == "e4m3":
        byte = np.frexp(amax)[1] - 1 + 127 - 7
    else:
        mant, ex = np.frexp(amax / 6.0)
        byte = np.where(mant > 0.5, ex, ex - 1) + 127
    byte = np.clip(np.where(amax > 0, byte, 1), 1, 254)
    scaled = (w * np.exp2(127.0 - byte)[:, None, :]).reshape(k, n).astype(np.float32)
    by_word = np.ascontiguousarray(scaled.reshape(k // 512, 128, 4, n).transpose(0, 1, 3, 2))
    if fmt == "e4m3":
        words = by_word.astype(ml_dtypes.float8_e4m3fn).view(np.uint8)
    else:
        c = by_word.astype(ml_dtypes.float4_e2m1fn).view(np.uint8) & 0xF
        words = (c[..., 0::2] | (c[..., 1::2] << 4)).reshape(k // 512, 128, 2 * n)
    return np.ascontiguousarray(words), np.ascontiguousarray(byte.astype(np.uint8).reshape(k // 512, 16, n))


def unpack_weight(words, scales, fmt):
    g, _, n = scales.shape
    words = np.ascontiguousarray(words).reshape(g, 128, n, -1)
    if fmt == "e4m3":
        vals = words.view(ml_dtypes.float8_e4m3fn).astype(np.float64)
    else:
        nib = np.empty((g, 128, n, 4), np.uint8)
        nib[..., 0::2] = words & 0xF
        nib[..., 1::2] = words >> 4
        vals = E2M1[nib]
    vals = vals * np.repeat(np.exp2(scales.astype(np.float64) - 127.0), 8, axis=1)[..., None]
    return vals.transpose(0, 1, 3, 2).reshape(g * 512, n)


def pack_table4(v):
    words, scales = pack_weight(v, "e2m1")
    g, t = words.shape[0] // 2, v.shape[1]
    return np.ascontiguousarray(words.reshape(g, 2, 128, t, 2).transpose(0, 2, 3, 1, 4).reshape(g, 128, t, 4)), scales


def unpack_table4(words, scales):
    g, _, t, _ = words.shape
    return unpack_weight(words.reshape(g, 128, t, 2, 2).transpose(0, 3, 1, 2, 4).reshape(2 * g, 128, 2 * t), scales, "e2m1")


K, L, R, N, T, J = 512, 1024, 512, 256, 2048, 1024


def setup_inputs():
    n = np.random.standard_normal
    s = mx_kscale(K)[:, None]
    s2 = mx_kscale(L)[:, None]
    u = mx_kscale(R)[:, None]
    p_tab = pack_weight(n((K, T)) * s, "e4m3")
    p_tab2 = pack_table4(n((L, T)) * s2)
    p_wer = pack_weight(n((K, R)) / np.sqrt(K) / s * u.T, "e2m1")
    p_wei = pack_weight(n((K, R)) / np.sqrt(K) / s * u.T, "e2m1")
    p_wrr = pack_weight(n((L, R)) / np.sqrt(L) / s2, "e2m1")
    p_wri = pack_weight(n((L, R)) / np.sqrt(L) / s2, "e2m1")
    p_nr = pack_weight(n((R, N)) / np.sqrt(R) / u, "e2m1")
    p_ni = pack_weight(n((R, N)) / np.sqrt(R) / u, "e2m1")
    return {
        "tab_words": p_tab[0],
        "tab_scales": p_tab[1],
        "tab2_words": p_tab2[0],
        "tab2_scales": p_tab2[1],
        "wer_words": p_wer[0],
        "wer_scales": p_wer[1],
        "wei_words": p_wei[0],
        "wei_scales": p_wei[1],
        "wrr_words": p_wrr[0],
        "wrr_scales": p_wrr[1],
        "wri_words": p_wri[0],
        "wri_scales": p_wri[1],
        "nr_words": p_nr[0],
        "nr_scales": p_nr[1],
        "ni_words": p_ni[0],
        "ni_scales": p_ni[1],
        "b": (0.3 * n(N)).astype(np.float32),
        "offs": striped(np.random.permutation(T)[:J]),
        "offs2": striped(np.random.permutation(T)[:J]),
    }


def reference(tab_words, tab_scales, tab2_words, tab2_scales, wer_words, wer_scales, wei_words, wei_scales, wrr_words, wrr_scales, wri_words, wri_scales, nr_words, nr_scales, ni_words, ni_scales, b, offs, offs2):
    idx = unstriped(offs)
    idx2 = unstriped(offs2)
    tab_ = unpack_weight(tab_words, tab_scales, "e4m3")[:, idx]
    tab2_ = unpack_table4(tab2_words, tab2_scales)[:, idx2]
    wer_ = unpack_weight(wer_words, wer_scales, "e2m1")
    aer = wer_.T @ tab_
    wei_ = unpack_weight(wei_words, wei_scales, "e2m1")
    aei = wei_.T @ tab_
    wrr_ = unpack_weight(wrr_words, wrr_scales, "e2m1")
    arr = wrr_.T @ tab2_
    wri_ = unpack_weight(wri_words, wri_scales, "e2m1")
    ari = wri_.T @ tab2_
    hr = aer * arr - aei * ari
    hi = aer * ari + aei * arr
    hr_ = mxq(hr, 0, "e4m3")
    hi_ = mxq(hi, 0, "e4m3")
    nr_ = unpack_weight(nr_words, nr_scales, "e2m1")
    ni_ = unpack_weight(ni_words, ni_scales, "e2m1")
    y = nr_.T @ hr_ + ni_.T @ hi_
    return y + f64(b)[:, None]

@@ -1,0 +1,250 @@
+from contextlib import ExitStack
+
+import concourse.mybir as mybir
+from concourse.masks import make_identity
+
+K, L, R, N, T, J = 512, 1024, 512, 256, 2048, 1024
+FLOPS = 2 * J * (2 * K * R + 2 * L * R + 2 * R * N)
+
+F32 = mybir.dt.float32
+BF16 = mybir.dt.bfloat16
+I32 = mybir.dt.int32
+U32 = mybir.dt.uint32
+U16 = mybir.dt.uint16
+U8 = mybir.dt.uint8
+FP8X4 = mybir.dt.float8_e4m3fn_x4
+FP4X4 = mybir.dt.float4_e2m1fn_x4
+MULT = mybir.AluOpType.mult
+IDENTITY = mybir.ActivationFunctionType.Identity
+
+P = 128
+TILES = J // P
+SHIFT_ROWS = 112
+
+
+def tile_list_ckg_bias_kernel(
+    tc, tab_words, tab_scales, tab2_words, tab2_scales, wer_words, wer_scales, wei_words, wei_scales,
+    wrr_words, wrr_scales, wri_words, wri_scales, nr_words, nr_scales, ni_words, ni_scales, b, offs, offs2, out,
+):
+    nc = tc.nc
+    with ExitStack() as ctx:
+        keep = ctx.enter_context(tc.tile_pool(name="keep", bufs=1))
+        work = ctx.enter_context(tc.tile_pool(name="work", bufs=3))
+        psum = ctx.enter_context(tc.psum_pool(name="psum", bufs=1))
+
+        list1 = keep.tile([P, J // 16], U16, name="list1")
+        list2 = keep.tile([P, J // 16], U16, name="list2")
+        t1w = keep.tile([P, T], I32, name="t1w", align_bytes=64)
+        t2w = keep.tile([P, T], I32, name="t2w", align_bytes=64)
+        t1s = keep.tile([P, T // 4], I32, name="t1s", align_bytes=64)
+        t2s = keep.tile([P, T // 4], I32, name="t2s", align_bytes=64)
+        g1w = keep.tile([P, J], U32, name="g1w", align_bytes=64)
+        g2w = keep.tile([P, J], U32, name="g2w", align_bytes=64)
+        g1s = keep.tile([P, J], U8, name="g1s", align_bytes=64)
+        g2s = keep.tile([P, J], U8, name="g2s", align_bytes=64)
+        g2s1 = keep.tile([P, J // 4], I32, name="g2s1", align_bytes=64)
+        parts = keep.tile([P, 2, 2 * J], U8, name="parts", align_bytes=64)
+        w_rr = keep.tile([P, 2, 2 * R], U8, name="w_rr", align_bytes=64)
+        w_ri = keep.tile([P, 2, 2 * R], U8, name="w_ri", align_bytes=64)
+        w_er = keep.tile([P, 2 * R], U8, name="w_er", align_bytes=64)
+        w_ei = keep.tile([P, 2 * R], U8, name="w_ei", align_bytes=64)
+        w_nr = keep.tile([P, 2 * N], U8, name="w_nr", align_bytes=64)
+        w_ni = keep.tile([P, 2 * N], U8, name="w_ni", align_bytes=64)
+        SW = 6 * R + 2 * N
+        staged = keep.tile([16, SW // 4], I32, name="staged", align_bytes=64)
+        wplanes = keep.tile([P, SW // 4], I32, name="wplanes", align_bytes=64)
+        bias = keep.tile([P, 2], F32, name="bias")
+        ident = keep.tile([P, P], F32, name="ident", align_bytes=64)
+
+        nc.vector.memset(t2s[:], 0)
+        nc.vector.memset(t1s[:], 0)
+        nc.vector.memset(wplanes[:], 0)
+        nc.vector.memset(g2s1[:], 0)
+        make_identity(nc, ident[:])
+
+        def words(ap):
+            return ap.bitcast(I32)
+
+        def stage(scales, col, width, passes):
+            dst = staged[:, col // 4 : (col + passes * width) // 4].rearrange("q (a c) -> q a c", a=passes)
+            nc.sync.dma_start(out=dst, in_=words(scales).rearrange("a q c -> q a c"))
+
+        nc.sync.dma_start(list2[:], offs2)
+        stage(wrr_scales, 0, R, 2)
+        stage(wri_scales, 2 * R, R, 2)
+        for q in range(4):
+            nc.sync.dma_start(out=t2s[32 * q : 32 * q + 8, :], in_=words(tab2_scales[:, 4 * q : 4 * q + 4, :]))
+        nc.sync.dma_start(out=t2w[:], in_=words(tab2_words[0].rearrange("p t i -> p (t i)")))
+        stage(wer_scales, 4 * R, R, 1)
+        stage(wei_scales, 5 * R, R, 1)
+        stage(nr_scales, 6 * R, N, 1)
+        stage(ni_scales, 6 * R + N, N, 1)
+        nc.sync.dma_start(list1[:], offs)
+        nc.sync.dma_start(out=words(w_rr[:]), in_=words(wrr_words).rearrange("a p c -> p a c"))
+        nc.sync.dma_start(out=words(w_ri[:]), in_=words(wri_words).rearrange("a p c -> p a c"))
+        for q in range(4):
+            nc.gpsimd.dma_start(out=t1s[32 * q : 32 * q + 4, :], in_=words(tab_scales[0, 4 * q : 4 * q + 4, :]))
+        for q in range(4):
+            nc.sync.dma_start(out=wplanes[32 * q : 32 * q + 4, :], in_=staged[4 * q : 4 * q + 4, :])
+        nc.sync.dma_start(out=t1w[:], in_=words(tab_words[0].rearrange("p t i -> p (t i)")))
+        nc.sync.dma_start(out=words(w_er[:]), in_=words(wer_words[0]))
+        nc.sync.dma_start(out=words(w_ei[:]), in_=words(wei_words[0]))
+        nc.gpsimd.dma_start(out=words(w_nr[:]), in_=words(nr_words[0]))
+        nc.gpsimd.dma_start(out=words(w_ni[:]), in_=words(ni_words[0]))
+        with nc.allow_non_contiguous_dma(reason="one bias value a partition"):
+            nc.gpsimd.dma_start(out=bias[:], in_=b.rearrange("(c p) -> p c", p=P))
+
+        wsc = wplanes[:].bitcast(U8)
+
+        def gather(dst, window, lst, j0, j1):
+            nc.vector.tensor_copy(dst[:, j0:j1], window.indirect(lst[:, j0 // 16 : j1 // 16]))
+
+        def gather_t2s(j0, j1):
+            gather(g2s, t2s[:].bitcast(U8), list2, j0, j1)
+            nc.scalar.dma_start(
+                out=g2s1[0:SHIFT_ROWS, j0 // 4 : j1 // 4], in_=g2s[4 : 4 + SHIFT_ROWS, j0:j1].bitcast(I32)
+            )
+
+        def gather_t2w(j0, j1):
+            gather(g2w, t2w[:].bitcast(U32), list2, j0, j1)
+
+        def part(j0, j1):
+            nc.vector.tensor_copy(
+                out=parts[:, :, 2 * j0 : 2 * j1].bitcast(U16),
+                in_=g2w[:, j0:j1].bitcast(U16).rearrange("p (j d) -> p d j", d=2),
+            )
+
+        def gather_t1s(j0, j1):
+            gather(g1s, t1s[:].bitcast(U8), list1, j0, j1)
+
+        def gather_t1w(j0, j1):
+            gather(g1w, t1w[:].bitcast(U32), list1, j0, j1)
+
+        rel = {}
+        ent = {}
+        prods = {}
+        hbf = {}
+        hq = {}
+
+        def by_slot(bank):
+            return bank[:].rearrange("p (m t) -> p t m", t=4)
+
+        def relation(i):
+            js = slice(i * P, (i + 1) * P)
+            rel[i] = work.tile([P, 2, 4, P], F32, name="rel", tag="rel", bufs=6, align_bytes=64)
+            planes = (g2s[:, js], g2s1[:].bitcast(U8)[:, js])
+            for c, w in enumerate((w_rr, w_ri)):
+                bank = psum.tile([P, R], F32, name="relbank", tag="relbank", bufs=2)
+                for a in range(2):
+                    col = (2 * c + a) * R
+                    nc.tensor.matmul_mx(
+                        out=bank[:],
+                        lhsT=parts[:, a, 2 * i * P : 2 * (i + 1) * P].bitcast(FP4X4),
+                        lhsT_scale=planes[a],
+                        rhs=w[:, a, :].bitcast(FP4X4),
+                        rhs_scale=wsc[:, col : col + R],
+                        start=(a == 0),
+                        stop=(a == 1),
+                    )
+                nc.scalar.copy(out=rel[i][:, c, :, :], in_=by_slot(bank))
+
+        def entity(i):
+            js = slice(i * P, (i + 1) * P)
+            ent[i] = []
+            for c, w in enumerate((w_er, w_ei)):
+                bank = psum.tile([P, R], F32, name="entbank", tag="entbank", bufs=3)
+                col = (4 + c) * R
+                nc.tensor.matmul_mx(
+                    out=bank[:],
+                    lhsT=g1w[:, js].bitcast(FP8X4),
+                    lhsT_scale=g1s[:, js],
+                    rhs=w[:].bitcast(FP4X4),
+                    rhs_scale=wsc[:, col : col + R],
+                    start=True,
+                    stop=True,
+                )
+                ent[i].append(bank)
+
+        def products(i):
+            prods[i] = work.tile([P, 4, 4, P], F32, name="prods", tag="prods", bufs=2, align_bytes=64)
+            er, ei = by_slot(ent[i][0]), by_slot(ent[i][1])
+            rr, ri = rel[i][:, 0, :, :], rel[i][:, 1, :, :]
+            nc.vector.tensor_tensor(prods[i][:, 0, :, :], er, rr, MULT)
+            nc.vector.scalar_tensor_tensor(prods[i][:, 1, :, :], ei, -1.0, ri, MULT, MULT)
+            nc.vector.tensor_tensor(prods[i][:, 2, :, :], er, ri, MULT)
+            nc.vector.tensor_tensor(prods[i][:, 3, :, :], ei, rr, MULT)
+
+        def turn(i):
+            hbf[i] = work.tile([P, 2, P, 4], BF16, name="hbf", tag="hbf", bufs=2, align_bytes=64)
+            for c in range(2):
+                bank = psum.tile([P, 4, P], F32, name="hbank", tag="hbank", bufs=2)
+                for t in range(4):
+                    for term in range(2):
+                        nc.tensor.matmul(
+                            bank[:, t, :], prods[i][:, 2 * c + term, t, :], ident[:],
+                            start=(term == 0), stop=(term == 1), is_transpose=True,
+                        )
+                nc.scalar.copy(out=hbf[i][:, c, :, :], in_=bank[:].rearrange("p t j -> p j t"))
+
+        def quantise(i):
+            codes = work.tile([P, 2 * P], U32, name="codes", tag="codes", bufs=2, align_bytes=64)
+            plane = work.tile([P, 2 * P], U8, name="plane", tag="plane", bufs=2, align_bytes=64)
+            nc.vector.quantize_mx(
+                out=codes[:].bitcast(FP8X4), scales=plane[:], in_=hbf[i][:].rearrange("p c j t -> p (c j t)")
+            )
+            hq[i] = (codes, plane)
+
+        def score(i):
+            codes, plane = hq[i]
+            bank = psum.tile([P, 2, P], F32, name="ybank", tag="ybank", bufs=1)
+            res = work.tile([P, 2, P], F32, name="res", tag="res", bufs=3)
+            for nt in range(2):
+                for c, w in enumerate((w_nr, w_ni)):
+                    col = 6 * R + c * N + nt * P
+                    nc.tensor.matmul_mx(
+                        out=bank[:, nt, :],
+                        lhsT=w[:, 2 * nt * P : 2 * (nt + 1) * P].bitcast(FP4X4),
+                        lhsT_scale=wsc[:, col : col + P],
+                        rhs=codes[:, c * P : (c + 1) * P].bitcast(FP8X4),
+                        rhs_scale=plane[:, c * P : (c + 1) * P],
+                        start=(c == 0),
+                        stop=(c == 1),
+                    )
+            for nt in range(2):
+                nc.scalar.activation(res[:, nt, :], bank[:, nt, :], IDENTITY, bias=bias[:, nt : nt + 1])
+            nc.sync.dma_start(
+                out=out[:, i * P : (i + 1) * P].rearrange("(c p) j -> p c j", p=P), in_=res[:]
+            )
+
+        gather_t2s(0, 512)
+        gather_t2s(512, 1024)
+        gather_t2w(0, 256)
+        gather_t2w(256, 512)
+        part(0, 256)
+        gather_t1s(0, 512)
+        part(256, 512)
+        relation(0)
+        relation(1)
+        gather_t1w(0, 256)
+        entity(0)
+        later = {
+            0: [lambda: gather_t1w(256, 512), lambda: gather_t2w(512, 768)],
+            1: [lambda: gather_t2w(768, 1024), lambda: part(512, 768)],
+            2: [lambda: gather_t1s(512, 1024), lambda: part(768, 1024), lambda: gather_t1w(512, 768)],
+            4: [lambda: gather_t1w(768, 1024)],
+        }
+        for i in range(TILES + 2):
+            if i < TILES:
+                products(i)
+            if 0 <= i - 1 < TILES:
+                quantise(i - 1)
+            for job in later.get(i, []):
+                job()
+            if i + 1 < TILES:
+                entity(i + 1)
+            if i + 2 < TILES:
+                relation(i + 2)
+            if 0 <= i - 1 < TILES:
+                score(i - 1)
+            if i < TILES:
+                turn(i)

@@ -34,91 +34,79 @@ def tile_list_ckg_bias_kernel(
 
         list1 = keep.tile([P, J // 16], U16, name="list1")
         list2 = keep.tile([P, J // 16], U16, name="list2")
-        t1w = keep.tile([P, T], I32, name="t1w", align_bytes=64)
         t2w = keep.tile([P, T], I32, name="t2w", align_bytes=64)
-        t1s = keep.tile([P, T // 4], I32, name="t1s", align_bytes=64)
-        t2s = keep.tile([P, T // 4], I32, name="t2s", align_bytes=64)
-        g1w = keep.tile([P, J], U32, name="g1w", align_bytes=64)
-        g2w = keep.tile([P, J], U32, name="g2w", align_bytes=64)
-        g1s = keep.tile([P, J], U8, name="g1s", align_bytes=64)
-        g2s = keep.tile([P, J], U8, name="g2s", align_bytes=64)
-        g2s1 = keep.tile([P, J // 4], I32, name="g2s1", align_bytes=64)
-        parts = keep.tile([P, 2, 2 * J], U8, name="parts", align_bytes=64)
-        w_rr = keep.tile([P, 2, 2 * R], U8, name="w_rr", align_bytes=64)
-        w_ri = keep.tile([P, 2, 2 * R], U8, name="w_ri", align_bytes=64)
-        w_er = keep.tile([P, 2 * R], U8, name="w_er", align_bytes=64)
-        w_ei = keep.tile([P, 2 * R], U8, name="w_ei", align_bytes=64)
-        w_nr = keep.tile([P, 2 * N], U8, name="w_nr", align_bytes=64)
-        w_ni = keep.tile([P, 2 * N], U8, name="w_ni", align_bytes=64)
+        t2s = work.tile([P, T // 4], I32, name="t2s", tag="window", bufs=1, align_bytes=64)
+        WS, SS = 256, 512
+        g1w = [keep.tile([P, WS], U32, name="g1w%d" % s, align_bytes=64) for s in range(J // WS)]
+        g2w = [work.tile([P, WS], U32, name="g2w%d" % s, tag="g2w%d" % s, bufs=1, align_bytes=64) for s in range(J // WS)]
+        parts = [keep.tile([P, 2, 2 * WS], U8, name="parts%d" % s, align_bytes=64) for s in range(J // WS)]
+        g1s = [keep.tile([P, SS], U8, name="g1s%d" % s, align_bytes=64) for s in range(J // SS)]
+        g2s = [keep.tile([P, SS], U8, name="g2s%d" % s, align_bytes=64) for s in range(J // SS)]
+        g2s1 = [keep.tile([P, SS // 4], I32, name="g2s1%d" % s, align_bytes=64) for s in range(J // SS)]
         SW = 6 * R + 2 * N
-        staged = keep.tile([16, SW // 4], I32, name="staged", align_bytes=64)
         wplanes = keep.tile([P, SW // 4], I32, name="wplanes", align_bytes=64)
-        bias = keep.tile([P, 2], F32, name="bias")
         ident = keep.tile([P, P], F32, name="ident", align_bytes=64)
-
-        nc.vector.memset(t2s[:], 0)
-        nc.vector.memset(t1s[:], 0)
-        nc.vector.memset(wplanes[:], 0)
-        nc.vector.memset(g2s1[:], 0)
-        make_identity(nc, ident[:])
 
         def words(ap):
             return ap.bitcast(I32)
 
+        nc.gpsimd.memset(t2s[:], 0)
+        nc.gpsimd.dma_start(out=t2w[:], in_=words(tab2_words[0].rearrange("p t i -> p (t i)")))
+        drawn = work.tile([P, P], F32, name="drawn", tag="w_rel", bufs=1, align_bytes=64)
+        make_identity(nc, drawn[:])
+        nc.scalar.copy(out=ident[:], in_=drawn[:])
+        nc.vector.memset(wplanes[:], 0)
+        for s in range(J // SS):
+            nc.vector.memset(g2s1[s][:], 0)
+
         def stage(scales, col, width, passes):
-            dst = staged[:, col // 4 : (col + passes * width) // 4].rearrange("q (a c) -> q a c", a=passes)
+            dst = wplanes[0:16, col // 4 : (col + passes * width) // 4].rearrange("q (a c) -> q a c", a=passes)
             nc.sync.dma_start(out=dst, in_=words(scales).rearrange("a q c -> q a c"))
 
         nc.sync.dma_start(list2[:], offs2)
+        nc.sync.dma_start(list1[:], offs)
+        t2rows = words(tab2_scales).rearrange("a (q r) c -> r q a c", r=4)
+        for r in range(4):
+            nc.sync.dma_start(out=t2s[r:P:16, :], in_=t2rows[r])
         stage(wrr_scales, 0, R, 2)
         stage(wri_scales, 2 * R, R, 2)
-        for q in range(4):
-            nc.sync.dma_start(out=t2s[32 * q : 32 * q + 8, :], in_=words(tab2_scales[:, 4 * q : 4 * q + 4, :]))
-        nc.sync.dma_start(out=t2w[:], in_=words(tab2_words[0].rearrange("p t i -> p (t i)")))
         stage(wer_scales, 4 * R, R, 1)
         stage(wei_scales, 5 * R, R, 1)
         stage(nr_scales, 6 * R, N, 1)
         stage(ni_scales, 6 * R + N, N, 1)
-        nc.sync.dma_start(list1[:], offs)
-        nc.sync.dma_start(out=words(w_rr[:]), in_=words(wrr_words).rearrange("a p c -> p a c"))
-        nc.sync.dma_start(out=words(w_ri[:]), in_=words(wri_words).rearrange("a p c -> p a c"))
-        for q in range(4):
-            nc.gpsimd.dma_start(out=t1s[32 * q : 32 * q + 4, :], in_=words(tab_scales[0, 4 * q : 4 * q + 4, :]))
-        for q in range(4):
-            nc.sync.dma_start(out=wplanes[32 * q : 32 * q + 4, :], in_=staged[4 * q : 4 * q + 4, :])
-        nc.sync.dma_start(out=t1w[:], in_=words(tab_words[0].rearrange("p t i -> p (t i)")))
-        nc.sync.dma_start(out=words(w_er[:]), in_=words(wer_words[0]))
-        nc.sync.dma_start(out=words(w_ei[:]), in_=words(wei_words[0]))
-        nc.gpsimd.dma_start(out=words(w_nr[:]), in_=words(nr_words[0]))
-        nc.gpsimd.dma_start(out=words(w_ni[:]), in_=words(ni_words[0]))
-        with nc.allow_non_contiguous_dma(reason="one bias value a partition"):
-            nc.gpsimd.dma_start(out=bias[:], in_=b.rearrange("(c p) -> p c", p=P))
+        w_rel = work.tile([P, 2, 2, 2 * R], U8, name="w_rel", tag="w_rel", bufs=1, align_bytes=64)
+        nc.sync.dma_start(out=words(w_rel[:, 0, :, :]), in_=words(wrr_words).rearrange("a p c -> p a c"))
+        nc.sync.dma_start(out=words(w_rel[:, 1, :, :]), in_=words(wri_words).rearrange("a p c -> p a c"))
+        for q in range(1, 4):
+            nc.sync.dma_start(out=wplanes[32 * q : 32 * q + 4, :], in_=wplanes[4 * q : 4 * q + 4, :])
 
         wsc = wplanes[:].bitcast(U8)
 
-        def gather(dst, window, lst, j0, j1):
-            nc.vector.tensor_copy(dst[:, j0:j1], window.indirect(lst[:, j0 // 16 : j1 // 16]))
+        def gather(dst, window, lst, s):
+            n = dst[s].shape[1] // 16
+            nc.vector.tensor_copy(dst[s][:], window.indirect(lst[:, s * n : (s + 1) * n]))
 
-        def gather_t2s(j0, j1):
-            gather(g2s, t2s[:].bitcast(U8), list2, j0, j1)
-            nc.scalar.dma_start(
-                out=g2s1[0:SHIFT_ROWS, j0 // 4 : j1 // 4], in_=g2s[4 : 4 + SHIFT_ROWS, j0:j1].bitcast(I32)
-            )
+        def gather_t2s(s):
+            gather(g2s, t2s[:].bitcast(U8), list2, s)
+            nc.sync.dma_start(out=g2s1[s][0:SHIFT_ROWS, :], in_=g2s[s][16:P, :].bitcast(I32))
 
-        def gather_t2w(j0, j1):
-            gather(g2w, t2w[:].bitcast(U32), list2, j0, j1)
+        def gather_t2w(s):
+            gather(g2w, t2w[:].bitcast(U32), list2, s)
 
-        def part(j0, j1):
+        def part(s):
             nc.vector.tensor_copy(
-                out=parts[:, :, 2 * j0 : 2 * j1].bitcast(U16),
-                in_=g2w[:, j0:j1].bitcast(U16).rearrange("p (j d) -> p d j", d=2),
+                out=parts[s][:].bitcast(U16), in_=g2w[s][:].bitcast(U16).rearrange("p (j d) -> p d j", d=2)
             )
 
-        def gather_t1s(j0, j1):
-            gather(g1s, t1s[:].bitcast(U8), list1, j0, j1)
+        def gather_t1s(s):
+            gather(g1s, t1s[:].bitcast(U8), list1, s)
 
-        def gather_t1w(j0, j1):
-            gather(g1w, t1w[:].bitcast(U32), list1, j0, j1)
+        def gather_t1w(s):
+            gather(g1w, t1w[:].bitcast(U32), list1, s)
+
+        def cols(tiles, i, width, per=1):
+            s, j0 = divmod(i * P, width)
+            return tiles[s], slice(per * j0, per * (j0 + P))
 
         rel = {}
         ent = {}
@@ -130,18 +118,20 @@ def tile_list_ckg_bias_kernel(
             return bank[:].rearrange("p (m t) -> p t m", t=4)
 
         def relation(i):
-            js = slice(i * P, (i + 1) * P)
-            rel[i] = work.tile([P, 2, 4, P], F32, name="rel", tag="rel", bufs=6, align_bytes=64)
-            planes = (g2s[:, js], g2s1[:].bitcast(U8)[:, js])
-            for c, w in enumerate((w_rr, w_ri)):
+            rel[i] = work.tile([P, 2, 4, P], F32, name="rel", tag="rel", bufs=8, align_bytes=64)
+            p0, js = cols(g2s, i, SS)
+            p1, js = cols(g2s1, i, SS)
+            planes = (p0[:, js], p1[:].bitcast(U8)[:, js])
+            pw, bs = cols(parts, i, WS, 2)
+            for c in range(2):
                 bank = psum.tile([P, R], F32, name="relbank", tag="relbank", bufs=2)
                 for a in range(2):
                     col = (2 * c + a) * R
                     nc.tensor.matmul_mx(
                         out=bank[:],
-                        lhsT=parts[:, a, 2 * i * P : 2 * (i + 1) * P].bitcast(FP4X4),
+                        lhsT=pw[:, a, bs].bitcast(FP4X4),
                         lhsT_scale=planes[a],
-                        rhs=w[:, a, :].bitcast(FP4X4),
+                        rhs=w_rel[:, c, a, :].bitcast(FP4X4),
                         rhs_scale=wsc[:, col : col + R],
                         start=(a == 0),
                         stop=(a == 1),
@@ -149,16 +139,17 @@ def tile_list_ckg_bias_kernel(
                 nc.scalar.copy(out=rel[i][:, c, :, :], in_=by_slot(bank))
 
         def entity(i):
-            js = slice(i * P, (i + 1) * P)
+            gw, jw = cols(g1w, i, WS)
+            gs, js = cols(g1s, i, SS)
             ent[i] = []
-            for c, w in enumerate((w_er, w_ei)):
+            for c in range(2):
                 bank = psum.tile([P, R], F32, name="entbank", tag="entbank", bufs=3)
                 col = (4 + c) * R
                 nc.tensor.matmul_mx(
                     out=bank[:],
-                    lhsT=g1w[:, js].bitcast(FP8X4),
-                    lhsT_scale=g1s[:, js],
-                    rhs=w[:].bitcast(FP4X4),
+                    lhsT=gw[:, jw].bitcast(FP8X4),
+                    lhsT_scale=gs[:, js],
+                    rhs=w_ent[:, c, :].bitcast(FP4X4),
                     rhs_scale=wsc[:, col : col + R],
                     start=True,
                     stop=True,
@@ -166,7 +157,7 @@ def tile_list_ckg_bias_kernel(
                 ent[i].append(bank)
 
         def products(i):
-            prods[i] = work.tile([P, 4, 4, P], F32, name="prods", tag="prods", bufs=2, align_bytes=64)
+            prods[i] = work.tile([P, 4, 4, P], F32, name="prods", tag="prods", bufs=3, align_bytes=64)
             er, ei = by_slot(ent[i][0]), by_slot(ent[i][1])
             rr, ri = rel[i][:, 0, :, :], rel[i][:, 1, :, :]
             nc.vector.tensor_tensor(prods[i][:, 0, :, :], er, rr, MULT)
@@ -199,11 +190,11 @@ def tile_list_ckg_bias_kernel(
             bank = psum.tile([P, 2, P], F32, name="ybank", tag="ybank", bufs=1)
             res = work.tile([P, 2, P], F32, name="res", tag="res", bufs=3)
             for nt in range(2):
-                for c, w in enumerate((w_nr, w_ni)):
+                for c in range(2):
                     col = 6 * R + c * N + nt * P
                     nc.tensor.matmul_mx(
                         out=bank[:, nt, :],
-                        lhsT=w[:, 2 * nt * P : 2 * (nt + 1) * P].bitcast(FP4X4),
+                        lhsT=w_cand[:, c, 2 * nt * P : 2 * (nt + 1) * P].bitcast(FP4X4),
                         lhsT_scale=wsc[:, col : col + P],
                         rhs=codes[:, c * P : (c + 1) * P].bitcast(FP8X4),
                         rhs_scale=plane[:, c * P : (c + 1) * P],
@@ -216,22 +207,41 @@ def tile_list_ckg_bias_kernel(
                 out=out[:, i * P : (i + 1) * P].rearrange("(c p) j -> p c j", p=P), in_=res[:]
             )
 
-        gather_t2s(0, 512)
-        gather_t2s(512, 1024)
-        gather_t2w(0, 256)
-        gather_t2w(256, 512)
-        part(0, 256)
-        gather_t1s(0, 512)
-        part(256, 512)
+        gather_t2s(0)
+        gather_t2s(1)
+        t1s = work.tile([P, T // 4], I32, name="t1s", tag="window", bufs=1, align_bytes=64)
+        nc.vector.memset(t1s[:], 0)
+        for q in range(4):
+            nc.sync.dma_start(out=t1s[32 * q : 32 * q + 4, :], in_=words(tab_scales[0, 4 * q : 4 * q + 4, :]))
+        gather_t2w(0)
+        gather_t2w(1)
+        part(0)
+        t1w = work.tile([P, T], I32, name="t1w", tag="g2w0", bufs=1, align_bytes=64)
+        nc.sync.dma_start(out=t1w[:], in_=words(tab_words[0].rearrange("p t i -> p (t i)")))
+        gather_t2w(2)
+        part(1)
+        w_ent = work.tile([P, 2, 2 * R], U8, name="w_ent", tag="g2w1", bufs=1, align_bytes=64)
+        nc.sync.dma_start(out=words(w_ent[:, 0, :]), in_=words(wer_words[0]))
+        nc.sync.dma_start(out=words(w_ent[:, 1, :]), in_=words(wei_words[0]))
         relation(0)
         relation(1)
-        gather_t1w(0, 256)
+        gather_t2w(3)
+        part(2)
+        gather_t1s(0)
+        part(3)
+        w_cand = work.tile([P, 2, 2 * N], U8, name="w_cand", tag="g2w2", bufs=1, align_bytes=64)
+        bias = work.tile([P, 2], F32, name="bias", tag="g2w3", bufs=1, align_bytes=64)
+        nc.sync.dma_start(out=words(w_cand[:, 0, :]), in_=words(nr_words[0]))
+        nc.sync.dma_start(out=words(w_cand[:, 1, :]), in_=words(ni_words[0]))
+        with nc.allow_non_contiguous_dma(reason="one bias value a partition"):
+            nc.sync.dma_start(out=bias[:], in_=b.rearrange("(c p) -> p c", p=P))
+        gather_t1w(0)
         entity(0)
         later = {
-            0: [lambda: gather_t1w(256, 512), lambda: gather_t2w(512, 768)],
-            1: [lambda: gather_t2w(768, 1024), lambda: part(512, 768)],
-            2: [lambda: gather_t1s(512, 1024), lambda: part(768, 1024), lambda: gather_t1w(512, 768)],
-            4: [lambda: gather_t1w(768, 1024)],
+            0: [lambda: gather_t1w(1)],
+            1: [lambda: gather_t1s(1)],
+            2: [lambda: gather_t1w(2)],
+            4: [lambda: gather_t1w(3)],
         }
         for i in range(TILES + 2):
             if i < TILES:

@@ -15,6 +15,7 @@ U8 = mybir.dt.uint8
 FP8X4 = mybir.dt.float8_e4m3fn_x4
 FP4X4 = mybir.dt.float4_e2m1fn_x4
 MULT = mybir.AluOpType.mult
+ADD = mybir.AluOpType.add
 IDENTITY = mybir.ActivationFunctionType.Identity
 
 P = 128
@@ -35,7 +36,7 @@ def tile_list_ckg_bias_kernel(
         list1 = keep.tile([P, J // 16], U16, name="list1")
         list2 = keep.tile([P, J // 16], U16, name="list2")
         t2w = keep.tile([P, T], I32, name="t2w", align_bytes=64)
-        t2s = work.tile([P, T // 4], I32, name="t2s", tag="window", bufs=1, align_bytes=64)
+        t2s = keep.tile([P, T // 4], I32, name="t2s", align_bytes=64)
         WS, SS = 256, 512
         g1w = [keep.tile([P, WS], U32, name="g1w%d" % s, align_bytes=64) for s in range(J // WS)]
         g2w = [work.tile([P, WS], U32, name="g2w%d" % s, tag="g2w%d" % s, bufs=1, align_bytes=64) for s in range(J // WS)]
@@ -50,35 +51,44 @@ def tile_list_ckg_bias_kernel(
         def words(ap):
             return ap.bitcast(I32)
 
+        t1w = keep.tile([P, T], I32, name="t1w", align_bytes=64)
+        t1s = keep.tile([P, T // 4], I32, name="t1s", align_bytes=64)
+        w_rel = keep.tile([P, 2, 2, 2 * R], U8, name="w_rel", align_bytes=64)
+        w_ent = keep.tile([P, 2, 2 * R], U8, name="w_ent", align_bytes=64)
         nc.gpsimd.memset(t2s[:], 0)
         nc.gpsimd.dma_start(out=t2w[:], in_=words(tab2_words[0].rearrange("p t i -> p (t i)")))
-        drawn = work.tile([P, P], F32, name="drawn", tag="w_rel", bufs=1, align_bytes=64)
-        make_identity(nc, drawn[:])
-        nc.scalar.copy(out=ident[:], in_=drawn[:])
-        nc.vector.memset(wplanes[:], 0)
+        nc.gpsimd.dma_start(out=words(w_rel[:, 0, :, :]), in_=words(wrr_words).rearrange("a p c -> p a c"))
+        nc.gpsimd.dma_start(out=words(w_rel[:, 1, :, :]), in_=words(wri_words).rearrange("a p c -> p a c"))
+        nc.gpsimd.dma_start(out=words(w_ent[:, 0, :]), in_=words(wer_words[0]))
+        nc.gpsimd.dma_start(out=t1w[:], in_=words(tab_words[0].rearrange("p t i -> p (t i)")))
+        nc.gpsimd.dma_start(out=words(w_ent[:, 1, :]), in_=words(wei_words[0]))
+        make_identity(nc, ident[:])
         for s in range(J // SS):
             nc.vector.memset(g2s1[s][:], 0)
+        nc.vector.memset(wplanes[:], 0)
+        nc.vector.memset(t1s[:], 0)
 
-        def stage(scales, col, width, passes):
+        queues = (nc.sync, nc.scalar)
+
+        def stage(queue, scales, col, width, passes):
             dst = wplanes[0:16, col // 4 : (col + passes * width) // 4].rearrange("q (a c) -> q a c", a=passes)
-            nc.sync.dma_start(out=dst, in_=words(scales).rearrange("a q c -> q a c"))
+            queue.dma_start(out=dst, in_=words(scales).rearrange("a q c -> q a c"))
 
         nc.sync.dma_start(list2[:], offs2)
         nc.sync.dma_start(list1[:], offs)
         t2rows = words(tab2_scales).rearrange("a (q r) c -> r q a c", r=4)
         for r in range(4):
-            nc.sync.dma_start(out=t2s[r:P:16, :], in_=t2rows[r])
-        stage(wrr_scales, 0, R, 2)
-        stage(wri_scales, 2 * R, R, 2)
-        stage(wer_scales, 4 * R, R, 1)
-        stage(wei_scales, 5 * R, R, 1)
-        stage(nr_scales, 6 * R, N, 1)
-        stage(ni_scales, 6 * R + N, N, 1)
-        w_rel = work.tile([P, 2, 2, 2 * R], U8, name="w_rel", tag="w_rel", bufs=1, align_bytes=64)
-        nc.sync.dma_start(out=words(w_rel[:, 0, :, :]), in_=words(wrr_words).rearrange("a p c -> p a c"))
-        nc.sync.dma_start(out=words(w_rel[:, 1, :, :]), in_=words(wri_words).rearrange("a p c -> p a c"))
+            queues[r % 2].dma_start(out=t2s[r:P:16, :], in_=t2rows[r])
+        stage(nc.sync, wrr_scales, 0, R, 2)
+        stage(nc.scalar, wri_scales, 2 * R, R, 2)
+        stage(nc.sync, wer_scales, 4 * R, R, 1)
+        stage(nc.scalar, wei_scales, 5 * R, R, 1)
+        stage(nc.sync, nr_scales, 6 * R, N, 1)
+        stage(nc.scalar, ni_scales, 6 * R + N, N, 1)
+        for q in range(4):
+            queues[q % 2].dma_start(out=t1s[32 * q : 32 * q + 4, :], in_=words(tab_scales[0, 4 * q : 4 * q + 4, :]))
         for q in range(1, 4):
-            nc.sync.dma_start(out=wplanes[32 * q : 32 * q + 4, :], in_=wplanes[4 * q : 4 * q + 4, :])
+            nc.scalar.dma_start(out=wplanes[32 * q : 32 * q + 4, :], in_=wplanes[4 * q : 4 * q + 4, :])
 
         wsc = wplanes[:].bitcast(U8)
 
@@ -111,6 +121,7 @@ def tile_list_ckg_bias_kernel(
         rel = {}
         ent = {}
         prods = {}
+        his = {}
         hbf = {}
         hq = {}
 
@@ -156,26 +167,37 @@ def tile_list_ckg_bias_kernel(
                 )
                 ent[i].append(bank)
 
+        def by_pair(bank):
+            return bank[:].rearrange("p (m u e) -> p u m e", u=2, e=2)
+
         def products(i):
-            prods[i] = work.tile([P, 4, 4, P], F32, name="prods", tag="prods", bufs=3, align_bytes=64)
-            er, ei = by_slot(ent[i][0]), by_slot(ent[i][1])
+            prods[i] = work.tile([P, 2, 4, P], F32, name="prods", tag="prods", bufs=3, align_bytes=64)
+            terms = work.tile([P, 2, 2, P, 2], F32, name="terms", tag="terms", bufs=2, align_bytes=64)
+            his[i] = work.tile([P, R], BF16, name="his", tag="his", bufs=3, align_bytes=64)
+            er, ei = ent[i]
             rr, ri = rel[i][:, 0, :, :], rel[i][:, 1, :, :]
-            nc.vector.tensor_tensor(prods[i][:, 0, :, :], er, rr, MULT)
-            nc.vector.scalar_tensor_tensor(prods[i][:, 1, :, :], ei, -1.0, ri, MULT, MULT)
-            nc.vector.tensor_tensor(prods[i][:, 2, :, :], er, ri, MULT)
-            nc.vector.tensor_tensor(prods[i][:, 3, :, :], ei, rr, MULT)
+            nc.vector.tensor_tensor(terms[:, 0, :, :, :], by_pair(er), ri.rearrange("p (u e) m -> p u m e", e=2), MULT)
+            nc.vector.tensor_tensor(terms[:, 1, :, :, :], by_pair(ei), rr.rearrange("p (u e) m -> p u m e", e=2), MULT)
+            flat = terms[:].rearrange("p c u m e -> p c (u m e)")
+            nc.gpsimd.tensor_tensor(his[i][:], flat[:, 0, :], flat[:, 1, :], ADD)
+            nc.vector.tensor_tensor(prods[i][:, 0, :, :], by_slot(er), rr, MULT)
+            nc.vector.scalar_tensor_tensor(prods[i][:, 1, :, :], by_slot(ei), -1.0, ri, MULT, MULT)
 
         def turn(i):
             hbf[i] = work.tile([P, 2, P, 4], BF16, name="hbf", tag="hbf", bufs=2, align_bytes=64)
-            for c in range(2):
-                bank = psum.tile([P, 4, P], F32, name="hbank", tag="hbank", bufs=2)
-                for t in range(4):
-                    for term in range(2):
-                        nc.tensor.matmul(
-                            bank[:, t, :], prods[i][:, 2 * c + term, t, :], ident[:],
-                            start=(term == 0), stop=(term == 1), is_transpose=True,
-                        )
-                nc.scalar.copy(out=hbf[i][:, c, :, :], in_=bank[:].rearrange("p t j -> p j t"))
+            bank = psum.tile([P, 4, P], F32, name="hbank", tag="hbank", bufs=2)
+            for t in range(4):
+                for term in range(2):
+                    nc.tensor.matmul(
+                        bank[:, t, :], prods[i][:, term, t, :], ident[:],
+                        start=(term == 0), stop=(term == 1), is_transpose=True,
+                    )
+            nc.scalar.copy(out=hbf[i][:, 0, :, :], in_=bank[:].rearrange("p t j -> p j t"))
+            bank = psum.tile([P, 2, P], F32, name="hbank", tag="hbank", bufs=2)
+            pairs = his[i][:].bitcast(F32)
+            for u in range(2):
+                nc.tensor.transpose(bank[:, u, :], pairs[:, u * P : (u + 1) * P], ident[:])
+            nc.scalar.copy(out=hbf[i][:, 1, :, :].bitcast(F32), in_=bank[:].rearrange("p u j -> p j u"))
 
         def quantise(i):
             codes = work.tile([P, 2 * P], U32, name="codes", tag="codes", bufs=2, align_bytes=64)
@@ -209,20 +231,11 @@ def tile_list_ckg_bias_kernel(
 
         gather_t2s(0)
         gather_t2s(1)
-        t1s = work.tile([P, T // 4], I32, name="t1s", tag="window", bufs=1, align_bytes=64)
-        nc.vector.memset(t1s[:], 0)
-        for q in range(4):
-            nc.sync.dma_start(out=t1s[32 * q : 32 * q + 4, :], in_=words(tab_scales[0, 4 * q : 4 * q + 4, :]))
         gather_t2w(0)
         gather_t2w(1)
         part(0)
-        t1w = work.tile([P, T], I32, name="t1w", tag="g2w0", bufs=1, align_bytes=64)
-        nc.sync.dma_start(out=t1w[:], in_=words(tab_words[0].rearrange("p t i -> p (t i)")))
         gather_t2w(2)
         part(1)
-        w_ent = work.tile([P, 2, 2 * R], U8, name="w_ent", tag="g2w1", bufs=1, align_bytes=64)
-        nc.sync.dma_start(out=words(w_ent[:, 0, :]), in_=words(wer_words[0]))
-        nc.sync.dma_start(out=words(w_ent[:, 1, :]), in_=words(wei_words[0]))
         relation(0)
         relation(1)
         gather_t2w(3)

@@ -177,6 +177,8 @@ def tile_list_ckg_bias_kernel(
             er, ei = ent[i]
             rr, ri = rel[i][:, 0, :, :], rel[i][:, 1, :, :]
             nc.vector.tensor_tensor(terms[:, 0, :, :, :], by_pair(er), ri.rearrange("p (u e) m -> p u m e", e=2), MULT)
+            if i >= 2:
+                quantise(i - 2)
             nc.vector.tensor_tensor(terms[:, 1, :, :, :], by_pair(ei), rr.rearrange("p (u e) m -> p u m e", e=2), MULT)
             flat = terms[:].rearrange("p c u m e -> p c (u m e)")
             nc.gpsimd.tensor_tensor(his[i][:], flat[:, 0, :], flat[:, 1, :], ADD)
@@ -184,7 +186,12 @@ def tile_list_ckg_bias_kernel(
             nc.vector.scalar_tensor_tensor(prods[i][:, 1, :, :], by_slot(ei), -1.0, ri, MULT, MULT)
 
         def turn(i):
-            hbf[i] = work.tile([P, 2, P, 4], BF16, name="hbf", tag="hbf", bufs=2, align_bytes=64)
+            hbf[i] = work.tile([P, 2, P, 4], BF16, name="hbf", tag="hbf", bufs=3, align_bytes=64)
+            bank = psum.tile([P, 2, P], F32, name="hbank", tag="hbank", bufs=2)
+            pairs = his[i][:].bitcast(F32)
+            for u in range(2):
+                nc.tensor.transpose(bank[:, u, :], pairs[:, u * P : (u + 1) * P], ident[:])
+            nc.scalar.copy(out=hbf[i][:, 1, :, :].bitcast(F32), in_=bank[:].rearrange("p u j -> p j u"))
             bank = psum.tile([P, 4, P], F32, name="hbank", tag="hbank", bufs=2)
             for t in range(4):
                 for term in range(2):
@@ -193,11 +200,6 @@ def tile_list_ckg_bias_kernel(
                         start=(term == 0), stop=(term == 1), is_transpose=True,
                     )
             nc.scalar.copy(out=hbf[i][:, 0, :, :], in_=bank[:].rearrange("p t j -> p j t"))
-            bank = psum.tile([P, 2, P], F32, name="hbank", tag="hbank", bufs=2)
-            pairs = his[i][:].bitcast(F32)
-            for u in range(2):
-                nc.tensor.transpose(bank[:, u, :], pairs[:, u * P : (u + 1) * P], ident[:])
-            nc.scalar.copy(out=hbf[i][:, 1, :, :].bitcast(F32), in_=bank[:].rearrange("p u j -> p j u"))
 
         def quantise(i):
             codes = work.tile([P, 2 * P], U32, name="codes", tag="codes", bufs=2, align_bytes=64)
@@ -248,26 +250,20 @@ def tile_list_ckg_bias_kernel(
         nc.sync.dma_start(out=words(w_cand[:, 1, :]), in_=words(ni_words[0]))
         with nc.allow_non_contiguous_dma(reason="one bias value a partition"):
             nc.sync.dma_start(out=bias[:], in_=b.rearrange("(c p) -> p c", p=P))
+        gather_t1s(1)
         gather_t1w(0)
         entity(0)
-        later = {
-            0: [lambda: gather_t1w(1)],
-            1: [lambda: gather_t1s(1)],
-            2: [lambda: gather_t1w(2)],
-            4: [lambda: gather_t1w(3)],
-        }
-        for i in range(TILES + 2):
-            if i < TILES:
-                products(i)
-            if 0 <= i - 1 < TILES:
-                quantise(i - 1)
-            for job in later.get(i, []):
-                job()
+        for i in range(TILES):
+            products(i)
+            if i % 2 == 0 and i // 2 + 1 < J // WS:
+                gather_t1w(i // 2 + 1)
             if i + 1 < TILES:
                 entity(i + 1)
             if i + 2 < TILES:
                 relation(i + 2)
-            if 0 <= i - 1 < TILES:
-                score(i - 1)
-            if i < TILES:
-                turn(i)
+            if i >= 2:
+                score(i - 2)
+            turn(i)
+        for i in range(TILES - 2, TILES):
+            quantise(i)
+            score(i)

from contextlib import ExitStack

import concourse.mybir as mybir
from concourse.masks import make_identity

K, L, R, N, T, J = 512, 1024, 512, 256, 2048, 1024
FLOPS = 2 * J * (2 * K * R + 2 * L * R + 2 * R * N)

F32 = mybir.dt.float32
BF16 = mybir.dt.bfloat16
I32 = mybir.dt.int32
U32 = mybir.dt.uint32
U16 = mybir.dt.uint16
U8 = mybir.dt.uint8
FP8X4 = mybir.dt.float8_e4m3fn_x4
FP4X4 = mybir.dt.float4_e2m1fn_x4
MULT = mybir.AluOpType.mult
ADD = mybir.AluOpType.add
IDENTITY = mybir.ActivationFunctionType.Identity

P = 128
TILES = J // P
SHIFT_ROWS = 112


def tile_list_ckg_bias_kernel(
    tc, tab_words, tab_scales, tab2_words, tab2_scales, wer_words, wer_scales, wei_words, wei_scales,
    wrr_words, wrr_scales, wri_words, wri_scales, nr_words, nr_scales, ni_words, ni_scales, b, offs, offs2, out,
):
    nc = tc.nc
    with ExitStack() as ctx:
        keep = ctx.enter_context(tc.tile_pool(name="keep", bufs=1))
        work = ctx.enter_context(tc.tile_pool(name="work", bufs=3))
        psum = ctx.enter_context(tc.psum_pool(name="psum", bufs=1))

        list1 = keep.tile([P, J // 16], U16, name="list1")
        list2 = keep.tile([P, J // 16], U16, name="list2")
        t2w = keep.tile([P, T], I32, name="t2w", align_bytes=64)
        t2s = keep.tile([P, T // 4], I32, name="t2s", align_bytes=64)
        WS, SS = 256, 512
        g1w = [keep.tile([P, WS], U32, name="g1w%d" % s, align_bytes=64) for s in range(J // WS)]
        g2w = [work.tile([P, WS], U32, name="g2w%d" % s, tag="g2w%d" % s, bufs=1, align_bytes=64) for s in range(J // WS)]
        parts = [keep.tile([P, 2, 2 * WS], U8, name="parts%d" % s, align_bytes=64) for s in range(J // WS)]
        g1s = [keep.tile([P, SS], U8, name="g1s%d" % s, align_bytes=64) for s in range(J // SS)]
        g2s = [keep.tile([P, SS], U8, name="g2s%d" % s, align_bytes=64) for s in range(J // SS)]
        g2s1 = [keep.tile([P, SS // 4], I32, name="g2s1%d" % s, align_bytes=64) for s in range(J // SS)]
        SW = 6 * R + 2 * N
        wplanes = keep.tile([P, SW // 4], I32, name="wplanes", align_bytes=64)
        ident = keep.tile([P, P], F32, name="ident", align_bytes=64)

        def words(ap):
            return ap.bitcast(I32)

        t1w = keep.tile([P, T], I32, name="t1w", align_bytes=64)
        t1s = keep.tile([P, T // 4], I32, name="t1s", align_bytes=64)
        w_rel = keep.tile([P, 2, 2, 2 * R], U8, name="w_rel", align_bytes=64)
        w_ent = keep.tile([P, 2, 2 * R], U8, name="w_ent", align_bytes=64)
        nc.gpsimd.memset(t2s[:], 0)
        nc.gpsimd.dma_start(out=t2w[:], in_=words(tab2_words[0].rearrange("p t i -> p (t i)")))
        nc.gpsimd.dma_start(out=words(w_rel[:, 0, :, :]), in_=words(wrr_words).rearrange("a p c -> p a c"))
        nc.gpsimd.dma_start(out=words(w_rel[:, 1, :, :]), in_=words(wri_words).rearrange("a p c -> p a c"))
        nc.gpsimd.dma_start(out=words(w_ent[:, 0, :]), in_=words(wer_words[0]))
        nc.gpsimd.dma_start(out=t1w[:], in_=words(tab_words[0].rearrange("p t i -> p (t i)")))
        nc.gpsimd.dma_start(out=words(w_ent[:, 1, :]), in_=words(wei_words[0]))
        make_identity(nc, ident[:])
        for s in range(J // SS):
            nc.vector.memset(g2s1[s][:], 0)
        nc.vector.memset(wplanes[:], 0)
        nc.vector.memset(t1s[:], 0)

        queues = (nc.sync, nc.scalar)

        def stage(queue, scales, col, width, passes):
            dst = wplanes[0:16, col // 4 : (col + passes * width) // 4].rearrange("q (a c) -> q a c", a=passes)
            queue.dma_start(out=dst, in_=words(scales).rearrange("a q c -> q a c"))

        nc.sync.dma_start(list2[:], offs2)
        nc.sync.dma_start(list1[:], offs)
        t2rows = words(tab2_scales).rearrange("a (q r) c -> r q a c", r=4)
        for r in range(4):
            queues[r % 2].dma_start(out=t2s[r:P:16, :], in_=t2rows[r])
        stage(nc.sync, wrr_scales, 0, R, 2)
        stage(nc.scalar, wri_scales, 2 * R, R, 2)
        stage(nc.sync, wer_scales, 4 * R, R, 1)
        stage(nc.scalar, wei_scales, 5 * R, R, 1)
        stage(nc.sync, nr_scales, 6 * R, N, 1)
        stage(nc.scalar, ni_scales, 6 * R + N, N, 1)
        for q in range(4):
            queues[q % 2].dma_start(out=t1s[32 * q : 32 * q + 4, :], in_=words(tab_scales[0, 4 * q : 4 * q + 4, :]))
        for q in range(1, 4):
            nc.scalar.dma_start(out=wplanes[32 * q : 32 * q + 4, :], in_=wplanes[4 * q : 4 * q + 4, :])

        wsc = wplanes[:].bitcast(U8)

        def gather(dst, window, lst, s):
            n = dst[s].shape[1] // 16
            nc.vector.tensor_copy(dst[s][:], window.indirect(lst[:, s * n : (s + 1) * n]))

        def gather_t2s(s):
            gather(g2s, t2s[:].bitcast(U8), list2, s)
            nc.sync.dma_start(out=g2s1[s][0:SHIFT_ROWS, :], in_=g2s[s][16:P, :].bitcast(I32))

        def gather_t2w(s):
            gather(g2w, t2w[:].bitcast(U32), list2, s)

        def part(s):
            nc.vector.tensor_copy(
                out=parts[s][:].bitcast(U16), in_=g2w[s][:].bitcast(U16).rearrange("p (j d) -> p d j", d=2)
            )

        def gather_t1s(s):
            gather(g1s, t1s[:].bitcast(U8), list1, s)

        def gather_t1w(s):
            gather(g1w, t1w[:].bitcast(U32), list1, s)

        def cols(tiles, i, width, per=1):
            s, j0 = divmod(i * P, width)
            return tiles[s], slice(per * j0, per * (j0 + P))

        rel = {}
        ent = {}
        prods = {}
        his = {}
        hbf = {}
        hq = {}

        def by_slot(bank):
            return bank[:].rearrange("p (m t) -> p t m", t=4)

        def relation(i):
            rel[i] = work.tile([P, 2, 4, P], F32, name="rel", tag="rel", bufs=8, align_bytes=64)
            p0, js = cols(g2s, i, SS)
            p1, js = cols(g2s1, i, SS)
            planes = (p0[:, js], p1[:].bitcast(U8)[:, js])
            pw, bs = cols(parts, i, WS, 2)
            for c in range(2):
                bank = psum.tile([P, R], F32, name="relbank", tag="relbank", bufs=2)
                for a in range(2):
                    col = (2 * c + a) * R
                    nc.tensor.matmul_mx(
                        out=bank[:],
                        lhsT=pw[:, a, bs].bitcast(FP4X4),
                        lhsT_scale=planes[a],
                        rhs=w_rel[:, c, a, :].bitcast(FP4X4),
                        rhs_scale=wsc[:, col : col + R],
                        start=(a == 0),
                        stop=(a == 1),
                    )
                nc.scalar.copy(out=rel[i][:, c, :, :], in_=by_slot(bank))

        def entity(i):
            gw, jw = cols(g1w, i, WS)
            gs, js = cols(g1s, i, SS)
            ent[i] = []
            for c in range(2):
                bank = psum.tile([P, R], F32, name="entbank", tag="entbank", bufs=3)
                col = (4 + c) * R
                nc.tensor.matmul_mx(
                    out=bank[:],
                    lhsT=gw[:, jw].bitcast(FP8X4),
                    lhsT_scale=gs[:, js],
                    rhs=w_ent[:, c, :].bitcast(FP4X4),
                    rhs_scale=wsc[:, col : col + R],
                    start=True,
                    stop=True,
                )
                ent[i].append(bank)

        def by_pair(bank):
            return bank[:].rearrange("p (m u e) -> p u m e", u=2, e=2)

        def products(i):
            prods[i] = work.tile([P, 2, 4, P], F32, name="prods", tag="prods", bufs=3, align_bytes=64)
            terms = work.tile([P, 2, 2, P, 2], F32, name="terms", tag="terms", bufs=2, align_bytes=64)
            his[i] = work.tile([P, R], BF16, name="his", tag="his", bufs=3, align_bytes=64)
            er, ei = ent[i]
            rr, ri = rel[i][:, 0, :, :], rel[i][:, 1, :, :]
            nc.vector.tensor_tensor(terms[:, 0, :, :, :], by_pair(er), ri.rearrange("p (u e) m -> p u m e", e=2), MULT)
            if i >= 2:
                quantise(i - 2)
            nc.vector.tensor_tensor(terms[:, 1, :, :, :], by_pair(ei), rr.rearrange("p (u e) m -> p u m e", e=2), MULT)
            flat = terms[:].rearrange("p c u m e -> p c (u m e)")
            nc.gpsimd.tensor_tensor(his[i][:], flat[:, 0, :], flat[:, 1, :], ADD)
            nc.vector.tensor_tensor(prods[i][:, 0, :, :], by_slot(er), rr, MULT)
            nc.vector.scalar_tensor_tensor(prods[i][:, 1, :, :], by_slot(ei), -1.0, ri, MULT, MULT)

        def turn(i):
            hbf[i] = work.tile([P, 2, P, 4], BF16, name="hbf", tag="hbf", bufs=3, align_bytes=64)
            bank = psum.tile([P, 2, P], F32, name="hbank", tag="hbank", bufs=2)
            pairs = his[i][:].bitcast(F32)
            for u in range(2):
                nc.tensor.transpose(bank[:, u, :], pairs[:, u * P : (u + 1) * P], ident[:])
            nc.scalar.copy(out=hbf[i][:, 1, :, :].bitcast(F32), in_=bank[:].rearrange("p u j -> p j u"))
            bank = psum.tile([P, 4, P], F32, name="hbank", tag="hbank", bufs=2)
            for t in range(4):
                for term in range(2):
                    nc.tensor.matmul(
                        bank[:, t, :], prods[i][:, term, t, :], ident[:],
                        start=(term == 0), stop=(term == 1), is_transpose=True,
                    )
            nc.scalar.copy(out=hbf[i][:, 0, :, :], in_=bank[:].rearrange("p t j -> p j t"))

        def quantise(i):
            codes = work.tile([P, 2 * P], U32, name="codes", tag="codes", bufs=2, align_bytes=64)
            plane = work.tile([P, 2 * P], U8, name="plane", tag="plane", bufs=2, align_bytes=64)
            nc.vector.quantize_mx(
                out=codes[:].bitcast(FP8X4), scales=plane[:], in_=hbf[i][:].rearrange("p c j t -> p (c j t)")
            )
            hq[i] = (codes, plane)

        def score(i):
            codes, plane = hq[i]
            bank = psum.tile([P, 2, P], F32, name="ybank", tag="ybank", bufs=1)
            res = work.tile([P, 2, P], F32, name="res", tag="res", bufs=3)
            for nt in range(2):
                for c in range(2):
                    col = 6 * R + c * N + nt * P
                    nc.tensor.matmul_mx(
                        out=bank[:, nt, :],
                        lhsT=w_cand[:, c, 2 * nt * P : 2 * (nt + 1) * P].bitcast(FP4X4),
                        lhsT_scale=wsc[:, col : col + P],
                        rhs=codes[:, c * P : (c + 1) * P].bitcast(FP8X4),
                        rhs_scale=plane[:, c * P : (c + 1) * P],
                        start=(c == 0),
                        stop=(c == 1),
                    )
            for nt in range(2):
                nc.scalar.activation(res[:, nt, :], bank[:, nt, :], IDENTITY, bias=bias[:, nt : nt + 1])
            nc.sync.dma_start(
                out=out[:, i * P : (i + 1) * P].rearrange("(c p) j -> p c j", p=P), in_=res[:]
            )

        gather_t2s(0)
        gather_t2s(1)
        gather_t2w(0)
        gather_t2w(1)
        part(0)
        gather_t2w(2)
        part(1)
        relation(0)
        relation(1)
        gather_t2w(3)
        part(2)
        gather_t1s(0)
        part(3)
        w_cand = work.tile([P, 2, 2 * N], U8, name="w_cand", tag="g2w2", bufs=1, align_bytes=64)
        bias = work.tile([P, 2], F32, name="bias", tag="g2w3", bufs=1, align_bytes=64)
        nc.sync.dma_start(out=words(w_cand[:, 0, :]), in_=words(nr_words[0]))
        nc.sync.dma_start(out=words(w_cand[:, 1, :]), in_=words(ni_words[0]))
        with nc.allow_non_contiguous_dma(reason="one bias value a partition"):
            nc.sync.dma_start(out=bias[:], in_=b.rearrange("(c p) -> p c", p=P))
        gather_t1s(1)
        gather_t1w(0)
        entity(0)
        for i in range(TILES):
            products(i)
            if i % 2 == 0 and i // 2 + 1 < J // WS:
                gather_t1w(i // 2 + 1)
            if i + 1 < TILES:
                entity(i + 1)
            if i + 2 < TILES:
                relation(i + 2)
            if i >= 2:
                score(i - 2)
            turn(i)
        for i in range(TILES - 2, TILES):
            quantise(i)
            score(i)
